import numpy as np, ml_dtypes
CORES = [0,1,2,3,4,5,6,7]
N = 8
WIDTHS = [12,48,6,96,0,48,12,6]
OFF = [0,12,60,66,162,162,210,222]
C = 228
def setup_inputs(rng):
    return {"x": rng.standard_normal((N, 128, C), dtype=np.float32).astype(ml_dtypes.bfloat16)}
def reference(x):
    s = x.sum(axis=0, dtype=np.float64).astype(x.dtype)
    YW = max(WIDTHS)
    y = np.full((N, 128, YW), np.nan, x.dtype)
    for r in range(N):
        y[r][:, :WIDTHS[r]] = s[:, OFF[r]:OFF[r] + WIDTHS[r]]
    return {"y": y}

@@ -1,0 +1,44 @@
+from concourse.mybir import AluOpType
+
+SCRATCH = {
+    "xs": ("sbuf", [128, 228], "bfloat16"),
+    "land": ("sbuf", [128, 8 * 96], "bfloat16"),
+}
+SEMAPHORES = ["loaded", "sent", "arrived", "added", "stored"]
+
+
+def rank_program(g, core, T, topo):
+    rank = T.rank_of(core)
+    if rank is None:
+        return
+    W = T.tables["WIDTHS"]
+    OFF = T.tables["OFF"]
+    n = len(W)
+    w = W[rank]
+    g.scalar.dma_start(T.xs[:], T.x[:]).then_inc(T.sem.loaded, 16)
+    if w:
+        g.sync.dma_start(T.land[:, rank * w:(rank + 1) * w],
+                         T.x[:, OFF[rank]:OFF[rank] + w]).then_inc(T.sem.arrived, 16)
+    g.wait_ge(T.sem.loaded, 16)
+    sent = 0
+    for k in range(1, n):
+        r = (rank + k) % n
+        if not W[r]:
+            continue
+        rid, pid, _se = topo.addr(T.cores[r])
+        g.remote_dma(T.land[:, rank * W[r]:(rank + 1) * W[r]], T.xs[:, OFF[r]:OFF[r] + W[r]],
+                     T.sem.arrived, T.sem.sent, pid, rid, topo.mask(core, T.cores[r]))
+        sent += 16
+    if w:
+        g.wait_ge(T.sem.arrived, 16 * n)
+        done = 0
+        h = n // 2
+        while h:
+            g.dma_start(T.land[:, 0:h * w], T.land[:, h * w:2 * h * w],
+                        accum_op=AluOpType.add).then_inc(T.sem.added, 16)
+            done += 16
+            g.wait_ge(T.sem.added, done)
+            h //= 2
+        g.dma_start(T.y[:, 0:w], T.land[:, 0:w]).then_inc(T.sem.stored, 16)
+        g.wait_ge(T.sem.stored, 16)
+    g.wait_ge(T.sem.sent, sent)

@@ -1,10 +1,36 @@
+from concourse.bass import DstId, RemoteDMATransfer
 from concourse.mybir import AluOpType
 
-SCRATCH = {
-    "xs": ("sbuf", [128, 228], "bfloat16"),
-    "land": ("sbuf", [128, 8 * 96], "bfloat16"),
+WIDTHS = (12, 48, 6, 96, 0, 48, 12, 6)
+CHUNKS = {
+    32: ((3, 0, 0), (3, 1, 2), (3, 2, 6)),
+    24: ((1, 0, 4), (1, 1, 5), (5, 0, 1), (5, 1, 7)),
+    12: ((0, 0, 3), (6, 0, 4)),
+    6: ((2, 0, 7), (7, 0, 3)),
 }
-SEMAPHORES = ["loaded", "sent", "arrived", "added", "stored"]
+SEND_ENGINES = {32: 4, 24: 4, 12: 8, 6: 8}
+PACK_ORDER = (3, 1, 5, 0, 6, 2, 7)
+CHUNK_WIDTH = {r: n for n in CHUNKS for (r, _t, _q) in CHUNKS[n]}
+
+SCRATCH = {}
+for _r in PACK_ORDER:
+    SCRATCH["blk%d" % _r] = ("dram", [WIDTHS[_r] // CHUNK_WIDTH[_r], 128, CHUNK_WIDTH[_r]], "bfloat16")
+for _n in CHUNKS:
+    SCRATCH["land%d" % _n] = ("dram", [6, 128, _n], "bfloat16")
+
+SEMAPHORES = ["pk%d" % _n for _n in CHUNKS] + ["arr%d" % _n for _n in CHUNKS] + ["summed", "sent", "stored"]
+
+
+def _reduced_by(q):
+    return [(n, r, t) for n in CHUNKS for (r, t, qq) in CHUNKS[n] if qq == q]
+
+
+def _fold_mask(q, j):
+    return 0xFFFF if len(_reduced_by(q)) == 1 else 0x00FF << (8 * j)
+
+
+def _engines(mask):
+    return bin(mask).count("1")
 
 
 def rank_program(g, core, T, topo):
@@ -13,32 +39,60 @@ def rank_program(g, core, T, topo):
         return
     W = T.tables["WIDTHS"]
     OFF = T.tables["OFF"]
-    n = len(W)
+    assert tuple(W) == WIDTHS
+    sem = T.sem
     w = W[rank]
-    g.scalar.dma_start(T.xs[:], T.x[:]).then_inc(T.sem.loaded, 16)
-    if w:
-        g.sync.dma_start(T.land[:, rank * w:(rank + 1) * w],
-                         T.x[:, OFF[rank]:OFF[rank] + w]).then_inc(T.sem.arrived, 16)
-    g.wait_ge(T.sem.loaded, 16)
-    sent = 0
-    for k in range(1, n):
-        r = (rank + k) % n
-        if not W[r]:
-            continue
+
+    def dst_id(r):
         rid, pid, _se = topo.addr(T.cores[r])
-        g.remote_dma(T.land[:, rank * W[r]:(rank + 1) * W[r]], T.xs[:, OFF[r]:OFF[r] + W[r]],
-                     T.sem.arrived, T.sem.sent, pid, rid, topo.mask(core, T.cores[r]))
-        sent += 16
+        return DstId(rid=rid, pnc=pid)
+
+    queues = (g.sync, g.scalar)
+    packed = {n: 0 for n in CHUNKS}
+    k = 0
+    for r in PACK_ORDER:
+        if r == rank:
+            continue
+        n = CHUNK_WIDTH[r]
+        queues[k % 2].dma_start(T["blk%d" % r][:], T.x[:, OFF[r]:OFF[r] + W[r]]).then_inc(sem["pk%d" % n], 16)
+        packed[n] += 16
+        k += 1
     if w:
-        g.wait_ge(T.sem.arrived, 16 * n)
-        done = 0
-        h = n // 2
-        while h:
-            g.dma_start(T.land[:, 0:h * w], T.land[:, h * w:2 * h * w],
-                        accum_op=AluOpType.add).then_inc(T.sem.added, 16)
-            done += 16
-            g.wait_ge(T.sem.added, done)
-            h //= 2
-        g.dma_start(T.y[:, 0:w], T.land[:, 0:w]).then_inc(T.sem.stored, 16)
-        g.wait_ge(T.sem.stored, 16)
-    g.wait_ge(T.sem.sent, sent)
+        queues[k % 2].dma_start(T.y[:, 0:w], T.x[:, OFF[rank]:OFF[rank] + w]).then_inc(sem.summed, 16)
+
+    sent = 0
+    for n in CHUNKS:
+        if packed[n]:
+            g.wait_ge(sem["pk%d" % n], packed[n])
+        e = SEND_ENGINES[n]
+        transfers = []
+        for i, (r, t, q) in enumerate(CHUNKS[n]):
+            if rank in (r, q):
+                continue
+            slot = [s for s in range(len(W)) if s not in (r, q)].index(rank)
+            transfers.append(RemoteDMATransfer(
+                dst_ids=[dst_id(q)], dma_engine_mask=((1 << e) - 1) << (e * i), remote_sem=sem["arr%d" % n],
+                src=T["blk%d" % r][t], dst=T["land%d" % n][slot]))
+            sent += e
+        if transfers:
+            g.remote_dma_fused(transfers, local_sem=sem.sent)
+
+    for j, (n, r, t) in enumerate(_reduced_by(rank)):
+        g.wait_ge(sem["arr%d" % n], 6 * SEND_ENGINES[n])
+        mask = _fold_mask(rank, j)
+        g.remote_dma_fused([RemoteDMATransfer(
+            dst_ids=[dst_id(r)], dma_engine_mask=mask, remote_sem=sem.summed,
+            srcs=[T["land%d" % n][s] for s in range(6)] + [T["blk%d" % r][t]], dsts=[T["blk%d" % r][t]],
+            alu_op=1)], local_sem=sem.sent)
+        sent += _engines(mask)
+
+    if w:
+        due = 16
+        for q in range(len(W)):
+            for j, (_n, r, _t) in enumerate(_reduced_by(q)):
+                if r == rank:
+                    due += _engines(_fold_mask(q, j))
+        g.wait_ge(sem.summed, due)
+        g.dma_start(T.y[:, 0:w], T["blk%d" % rank][:], accum_op=AluOpType.add).then_inc(sem.stored, 16)
+        g.wait_ge(sem.stored, 16)
+    g.wait_ge(sem.sent, sent)

from concourse.bass import DstId, RemoteDMATransfer
from concourse.mybir import AluOpType

WIDTHS = (12, 48, 6, 96, 0, 48, 12, 6)
CHUNKS = {
    32: ((3, 0, 0), (3, 1, 2), (3, 2, 6)),
    24: ((1, 0, 4), (1, 1, 5), (5, 0, 1), (5, 1, 7)),
    12: ((0, 0, 3), (6, 0, 4)),
    6: ((2, 0, 7), (7, 0, 3)),
}
SEND_ENGINES = {32: 4, 24: 4, 12: 8, 6: 8}
PACK_ORDER = (3, 1, 5, 0, 6, 2, 7)
CHUNK_WIDTH = {r: n for n in CHUNKS for (r, _t, _q) in CHUNKS[n]}

SCRATCH = {}
for _r in PACK_ORDER:
    SCRATCH["blk%d" % _r] = ("dram", [WIDTHS[_r] // CHUNK_WIDTH[_r], 128, CHUNK_WIDTH[_r]], "bfloat16")
for _n in CHUNKS:
    SCRATCH["land%d" % _n] = ("dram", [6, 128, _n], "bfloat16")

SEMAPHORES = ["pk%d" % _n for _n in CHUNKS] + ["arr%d" % _n for _n in CHUNKS] + ["summed", "sent", "stored"]


def _reduced_by(q):
    return [(n, r, t) for n in CHUNKS for (r, t, qq) in CHUNKS[n] if qq == q]


def _fold_mask(q, j):
    return 0xFFFF if len(_reduced_by(q)) == 1 else 0x00FF << (8 * j)


def _engines(mask):
    return bin(mask).count("1")


def rank_program(g, core, T, topo):
    rank = T.rank_of(core)
    if rank is None:
        return
    W = T.tables["WIDTHS"]
    OFF = T.tables["OFF"]
    assert tuple(W) == WIDTHS
    sem = T.sem
    w = W[rank]

    def dst_id(r):
        rid, pid, _se = topo.addr(T.cores[r])
        return DstId(rid=rid, pnc=pid)

    queues = (g.sync, g.scalar)
    packed = {n: 0 for n in CHUNKS}
    k = 0
    for r in PACK_ORDER:
        if r == rank:
            continue
        n = CHUNK_WIDTH[r]
        queues[k % 2].dma_start(T["blk%d" % r][:], T.x[:, OFF[r]:OFF[r] + W[r]]).then_inc(sem["pk%d" % n], 16)
        packed[n] += 16
        k += 1
    if w:
        queues[k % 2].dma_start(T.y[:, 0:w], T.x[:, OFF[rank]:OFF[rank] + w]).then_inc(sem.summed, 16)

    sent = 0
    for n in CHUNKS:
        if packed[n]:
            g.wait_ge(sem["pk%d" % n], packed[n])
        e = SEND_ENGINES[n]
        transfers = []
        for i, (r, t, q) in enumerate(CHUNKS[n]):
            if rank in (r, q):
                continue
            slot = [s for s in range(len(W)) if s not in (r, q)].index(rank)
            transfers.append(RemoteDMATransfer(
                dst_ids=[dst_id(q)], dma_engine_mask=((1 << e) - 1) << (e * i), remote_sem=sem["arr%d" % n],
                src=T["blk%d" % r][t], dst=T["land%d" % n][slot]))
            sent += e
        if transfers:
            g.remote_dma_fused(transfers, local_sem=sem.sent)

    for j, (n, r, t) in enumerate(_reduced_by(rank)):
        g.wait_ge(sem["arr%d" % n], 6 * SEND_ENGINES[n])
        mask = _fold_mask(rank, j)
        g.remote_dma_fused([RemoteDMATransfer(
            dst_ids=[dst_id(r)], dma_engine_mask=mask, remote_sem=sem.summed,
            srcs=[T["land%d" % n][s] for s in range(6)] + [T["blk%d" % r][t]], dsts=[T["blk%d" % r][t]],
            alu_op=1)], local_sem=sem.sent)
        sent += _engines(mask)

    if w:
        due = 16
        for q in range(len(W)):
            for j, (_n, r, _t) in enumerate(_reduced_by(q)):
                if r == rank:
                    due += _engines(_fold_mask(q, j))
        g.wait_ge(sem.summed, due)
        g.dma_start(T.y[:, 0:w], T["blk%d" % rank][:], accum_op=AluOpType.add).then_inc(sem.stored, 16)
        g.wait_ge(sem.stored, 16)
    g.wait_ge(sem.sent, sent)
